import numpy as np
import ml_dtypes


def mxq(x, axis, fmt="e4m3"):
    dtype, down = {"e4m3": (ml_dtypes.float8_e4m3fn, 7), "e5m2": (ml_dtypes.float8_e5m2, 14)}[fmt]
    v = np.moveaxis(np.asarray(x, np.float32).astype(ml_dtypes.bfloat16).astype(np.float64), axis, -1)
    blocks = v.reshape(v.shape[:-1] + (-1, 32))
    amax = np.abs(blocks).max(-1, keepdims=True)
    byte = np.maximum(np.where(amax > 0, np.frexp(amax)[1] - 1 + 127, 0) - down, 1)
    scale = np.exp2(byte - 127.0)
    codes = (blocks / scale).astype(np.float32).astype(dtype).astype(np.float64)
    return np.moveaxis((codes * scale).reshape(v.shape), -1, axis)


WIDE = False


def mx_kscale(k):
    if not WIDE:
        return np.ones(k)
    levels = np.array([10, -10, 5, -5, 0])
    if k % 512:
        return np.exp2(np.random.permutation(np.resize(levels, k // 32))).repeat(32)
    a = np.empty((k // 512, 16))
    for p in range(k // 512):
        a[p, :8] = np.random.permutation(np.resize(levels, 8))
        for g in range(8):
            far = levels[np.abs(levels - a[p, g]) >= 10]
            a[p, g + 8] = far[np.random.randint(len(far))]
    return np.exp2(a.ravel()).repeat(32)


def f64(x):
    return np.asarray(x).astype(np.float64)


def striped(idx):
    return np.tile(idx.reshape(-1, 16).T, (8, 1)).astype(np.uint16)


def unstriped(offs):
    return offs[:16].T.reshape(-1).astype(np.int64)


def pack_weight(w):
    k, n = w.shape
    w = f64(np.asarray(w, np.float32).astype(ml_dtypes.bfloat16)).reshape(k // 32, 32, n)
    amax = np.abs(w).max(1)
    byte = np.clip(np.where(amax > 0, np.frexp(amax)[1] - 1 + 127 - 7, 1), 1, 254)
    scaled = (w * np.exp2(127.0 - byte)[:, None, :]).reshape(k, n).astype(np.float32)
    words = np.ascontiguousarray(scaled.reshape(k // 512, 128, 4, n).transpose(0, 1, 3, 2)).astype(ml_dtypes.float8_e4m3fn).view(np.uint8)
    return words, np.ascontiguousarray(byte.astype(np.uint8).reshape(k // 512, 16, n))


def unpack_weight(words, scales):
    g, p, n, _ = words.shape
    vals = np.ascontiguousarray(words).view(ml_dtypes.float8_e4m3fn).astype(np.float64) * np.repeat(np.exp2(scales.astype(np.float64) - 127.0), 8, axis=1)[..., None]
    return vals.transpose(0, 1, 3, 2).reshape(g * 512, n)


K, T, S, N, H = 512, 2048, 512, 256, 512


def setup_inputs():
    n = np.random.standard_normal
    s = mx_kscale(K)[:, None]
    u = mx_kscale(H)
    packed_xT = pack_weight(n((K, T)) * s)
    return {
        "x_words": packed_xT[0],
        "x_scales": packed_xT[1],
        "w1": (n((K, H)) / np.sqrt(K) / s).astype(np.float32),
        "w2": (n((K, H)) / np.sqrt(K) / s).astype(np.float32),
        "ra": (n((H, S))).astype(np.float32),
        "rb": (n((H, S))).astype(np.float32),
        "unit": (np.random.uniform(0.6, 1.4, (H, 1)) * u[:, None]).astype(np.float32),
        "w3": (n((H, N)) / np.sqrt(H) / u[:, None]).astype(np.float32),
        "offs": striped(np.random.permutation(T)[:S]),
        "ant": striped(np.random.permutation(S)),
    }


def reference(x_words, x_scales, w1, w2, ra, rb, unit, w3, offs, ant):
    xq = unpack_weight(x_words, x_scales)[:, unstriped(offs)]
    hr = mxq(f64(w1), 0, "e4m3").T @ xq
    hi2 = mxq(f64(w2), 0, "e4m3").T @ xq
    gr = hr[:, unstriped(ant)]
    gi = hi2[:, unstriped(ant)]
    en = (hr) ** 2 + (hi2) ** 2 + (gr) ** 2 + (gi) ** 2 + 0.3
    sym1 = (hr * f64(ra) + gr * f64(rb) + 0.5 * (hi2 * f64(rb))) / en
    llr = (0.5 * np.sqrt(en)) * sym1
    sym2 = (gi * f64(ra) - (hi2 * f64(rb))) / en
    hid = f64(unit) * (llr + sym2)
    return mxq(f64(w3), 0, "e4m3").T @ mxq(hid, 0, "e4m3")

@@ -1,0 +1,241 @@
+from contextlib import ExitStack
+
+import concourse.mybir as mybir
+from concourse.masks import make_identity
+
+K, T, S, N, H = 512, 2048, 512, 256, 512
+FLOPS = 2 * K * H * S * 2 + 2 * H * N * S
+
+F32 = mybir.dt.float32
+BF16 = mybir.dt.bfloat16
+I32 = mybir.dt.int32
+U32 = mybir.dt.uint32
+U16 = mybir.dt.uint16
+U8 = mybir.dt.uint8
+FP8X4 = mybir.dt.float8_e4m3fn_x4
+ALU = mybir.AluOpType
+ACT = mybir.ActivationFunctionType
+
+P = 128
+PACK = 4
+HALF = 256
+LIST_COLS = HALF // 16
+
+
+def tile_picked_yalamo_lin_p_kernel(
+    tc, x_words, x_scales, w1, w2, ra, rb, unit, w3, offs, ant, out
+):
+    nc = tc.nc
+    with ExitStack() as ctx:
+        keep = ctx.enter_context(tc.tile_pool(name="keep", bufs=1))
+        work = ctx.enter_context(tc.tile_pool(name="work", bufs=2))
+        psum = ctx.enter_context(tc.psum_pool(name="psum", bufs=1))
+
+        offs_sb = keep.tile([P, S // 16], U16, name="offs_sb")
+        ant_sb = keep.tile([P, S // 16], U16, name="ant_sb")
+        table_words = keep.tile([P, T], I32, name="table_words", align_bytes=64)
+        table_scales = keep.tile([P, T], U8, name="table_scales", align_bytes=64)
+        unit_sb = keep.tile([P, 2, 2], F32, name="unit_sb")
+        ident = keep.tile([P, P], F32, name="ident")
+
+        def load_weight(w, c0, name):
+            raw = keep.tile([P, PACK, HALF], F32, name=name)
+            nc.sync.dma_start(out=raw[:], in_=w[:, c0 : c0 + HALF].rearrange("(p j) c -> p j c", j=PACK))
+            return raw
+
+        def load_received(r, h, name):
+            rows = keep.tile([P, 2, S], F32, name=name)
+            nc.sync.dma_start(out=rows[:], in_=r[h * HALF : (h + 1) * HALF, :].rearrange("(m u) c -> m u c", u=2))
+            return rows
+
+        nc.vector.memset(table_scales[:].bitcast(I32), 0)
+        nc.sync.dma_start(offs_sb[:], offs)
+        nc.sync.dma_start(out=table_words[:], in_=x_words[0].rearrange("p n t -> p (n t)").bitcast(I32))
+        for q in range(4):
+            nc.scalar.dma_start(
+                out=table_scales[32 * q : 32 * q + 4, :].bitcast(I32),
+                in_=x_scales[0, 4 * q : 4 * q + 4, :].bitcast(I32),
+            )
+        w1_raw, w2_raw, ra_sb, rb_sb = {}, {}, {}, {}
+        w1_raw[0] = load_weight(w1, 0, "w1_raw0")
+        w2_raw[0] = load_weight(w2, 0, "w2_raw0")
+        nc.sync.dma_start(ant_sb[:], ant)
+        nc.sync.dma_start(out=unit_sb[:], in_=unit.rearrange("(h m u) o -> m h (u o)", h=2, u=2))
+        ra_sb[0] = load_received(ra, 0, "ra0")
+        rb_sb[0] = load_received(rb, 0, "rb0")
+        w1_raw[1] = load_weight(w1, HALF, "w1_raw1")
+        w2_raw[1] = load_weight(w2, HALF, "w2_raw1")
+        ra_sb[1] = load_received(ra, 1, "ra1")
+        rb_sb[1] = load_received(rb, 1, "rb1")
+        w3_raw = load_weight(w3, 0, "w3_raw")
+        make_identity(nc, ident[:])
+
+        def quantize(grouped, name):
+            width = grouped.shape[1] // PACK
+            codes = keep.tile([P, width], U32, name=name + "_codes", align_bytes=64)
+            scales = keep.tile([P, width], U8, name=name + "_scales", align_bytes=64)
+            nc.vector.quantize_mx(out=codes[:].bitcast(FP8X4), scales=scales[:], in_=grouped[:])
+            return codes, scales
+
+        def prepare_first(raw, name, copy):
+            grouped = keep.tile([P, PACK * HALF], BF16, name=name + "_bf", align_bytes=64)
+            copy(
+                out=grouped[:].rearrange("p (u a l j) -> p a j l u", u=2, l=2, j=PACK),
+                in_=raw[:].rearrange("p j (a l u) -> p a j l u", l=2, u=2),
+            )
+            return quantize(grouped, name)
+
+        def prepare_last(raw, name, copy):
+            grouped = keep.tile([P, PACK * N], BF16, name=name + "_bf", align_bytes=64)
+            copy(
+                out=grouped[:].rearrange("p (a i u e) -> p a e u i", i=4, u=2, e=2),
+                in_=raw[:].rearrange("p (e u) (a i) -> p a e u i", u=2, i=4),
+            )
+            return quantize(grouped, name)
+
+        x_codes = keep.tile([P, S], U32, name="x_codes", align_bytes=64)
+        x_bytes = keep.tile([P, S], U8, name="x_bytes", align_bytes=64)
+        nc.vector.tensor_copy(x_bytes[:], table_scales[:].indirect(offs_sb[:]))
+        nc.vector.tensor_copy(x_codes[:], table_words[:].bitcast(U32).indirect(offs_sb[:]))
+
+        factor = keep.tile([P, 3, 4], F32, name="factor")
+        for n, c in enumerate((0.5, 0.25, -0.25)):
+            nc.vector.tensor_scalar(
+                factor[:, n, :], unit_sb[:].rearrange("p h u -> p (h u)"), c, 0.0, ALU.mult, ALU.add
+            )
+
+        def scalar_of(n, h, u):
+            return factor[:, n, 2 * h + u : 2 * h + u + 1]
+
+        def product(w, u, name):
+            codes, scales = w
+            bank = psum.tile([P, S], F32, name=name, tag="mm", bufs=3)
+            cols = slice(u * P, (u + 1) * P)
+            nc.tensor.matmul_mx(
+                out=bank[:], lhsT=codes[:, cols].bitcast(FP8X4), lhsT_scale=scales[:, cols],
+                rhs=x_codes[:].bitcast(FP8X4), rhs_scale=x_bytes[:], start=True, stop=True,
+            )
+            return bank
+
+        rows = {}
+
+        def channels(h, u, wq1, wq2):
+            name = "%d%d" % (h, u)
+            hr_ps = product(wq1, u, "hr_ps" + name)
+            hi_ps = product(wq2, u, "hi_ps" + name)
+            hr = keep.tile([P, S], F32, name="hr" + name)
+            hi = keep.tile([P, S], F32, name="hi" + name)
+            hr_sq = keep.tile([P, S], F32, name="hr_sq" + name)
+            hi_sq = keep.tile([P, S], F32, name="hi_sq" + name)
+            nc.scalar.copy(out=hr[:], in_=hr_ps[:])
+            nc.scalar.copy(out=hi[:], in_=hi_ps[:])
+            nc.scalar.activation(hr_sq[:], hr_ps[:], ACT.Square)
+            nc.scalar.activation(hi_sq[:], hi_ps[:], ACT.Square)
+            hr_ra = keep.tile([P, S], F32, name="hr_ra" + name)
+            hi_rb = keep.tile([P, S], F32, name="hi_rb" + name)
+            nc.vector.scalar_tensor_tensor(hr_ra[:], hr[:], scalar_of(0, h, u), ra_sb[h][:, u, :], ALU.mult, ALU.mult)
+            nc.vector.scalar_tensor_tensor(hi_rb[:], hi[:], scalar_of(2, h, u), rb_sb[h][:, u, :], ALU.mult, ALU.mult)
+            rows[h, u] = (hr, hi, hr_sq, hi_sq, hr_ra, hi_rb)
+
+        def add_turned(bank, n, terms):
+            for i, term in enumerate(terms):
+                nc.tensor.matmul(
+                    out=bank[:, n * P : (n + 1) * P], lhsT=term, rhs=ident[:],
+                    is_transpose=True, start=(i == 0), stop=(i == len(terms) - 1),
+                )
+
+        def front(h, s):
+            cols = slice(s * HALF, (s + 1) * HALF)
+            places = ant_sb[:, s * LIST_COLS : (s + 1) * LIST_COLS]
+            name = "%d%d" % (h, s)
+            en = psum.tile([P, S], F32, name="en" + name, tag="en", bufs=1)
+            ta = psum.tile([P, S], F32, name="ta" + name, tag="ta", bufs=2)
+            tb = psum.tile([P, S], F32, name="tb" + name, tag="tb", bufs=2)
+            made = []
+            for u in range(2):
+                hr, hi = rows[h, u][0], rows[h, u][1]
+                got = work.tile([P, 2, HALF], F32, name="got", tag="got%d" % u)
+                got_sq = work.tile([P, 2, HALF], F32, name="got_sq", tag="got_sq%d" % u)
+                gr_rb = work.tile([P, HALF], F32, name="gr_rb", tag="gr_rb%d" % u)
+                gi_ra = work.tile([P, HALF], F32, name="gi_ra", tag="gi_ra%d" % u)
+                nc.vector.tensor_copy(got[:, 0, :], hr[:].indirect(places))
+                nc.scalar.activation(got[:, 1, :], hi[:].indirect(places), ACT.Copy)
+                nc.scalar.activation(got_sq[:], got[:], ACT.Square)
+                nc.vector.scalar_tensor_tensor(gr_rb[:], got[:, 0, :], scalar_of(0, h, u), rb_sb[h][:, u, cols], ALU.mult, ALU.mult)
+                nc.vector.scalar_tensor_tensor(gi_ra[:], got[:, 1, :], scalar_of(1, h, u), ra_sb[h][:, u, cols], ALU.mult, ALU.mult)
+                made.append((got_sq, gr_rb, gi_ra))
+            blocks = [(u, b) for u in range(2) for b in range(2)]
+            for n, (u, b) in enumerate(blocks):
+                near = slice(b * P, (b + 1) * P)
+                far = slice(s * HALF + b * P, s * HALF + (b + 1) * P)
+                add_turned(en, n, [rows[h, u][2][:, far], rows[h, u][3][:, far], made[u][0][:, 0, near], made[u][0][:, 1, near]])
+            for n, (u, b) in enumerate(blocks):
+                near = slice(b * P, (b + 1) * P)
+                far = slice(s * HALF + b * P, s * HALF + (b + 1) * P)
+                add_turned(tb, n, [rows[h, u][5][:, far], made[u][2][:, near]])
+            for n, (u, b) in enumerate(blocks):
+                near = slice(b * P, (b + 1) * P)
+                far = slice(s * HALF + b * P, s * HALF + (b + 1) * P)
+                add_turned(ta, n, [rows[h, u][4][:, far], made[u][1][:, near], made[u][2][:, near]])
+            return en, ta, tb
+
+        hid_t = [keep.tile([P, 2, 2, HALF], BF16, name="hid_t%d" % s) for s in range(2)]
+
+        def back(h, s, banks):
+            en, ta, tb = banks
+            root = work.tile([P, S], F32, name="root")
+            part = work.tile([P, S], F32, name="part")
+            both = work.tile([P, S], F32, name="both")
+            nc.scalar.activation(root[:], en[:], ACT.Abs_reciprocal_sqrt, bias=0.3)
+            nc.vector.scalar_tensor_tensor(part[:], root[:], -0.25, tb[:], ALU.add, ALU.mult)
+            nc.vector.scalar_tensor_tensor(both[:], part[:], 4.0, ta[:], ALU.mult, ALU.add)
+            nc.vector.tensor_tensor(
+                hid_t[s][:, :, :, h * P : (h + 1) * P],
+                both[:].rearrange("p (u b m) -> p u b m", u=2, b=2),
+                root[:].rearrange("p (u b m) -> p u b m", u=2, b=2),
+                ALU.mult,
+            )
+
+        def streams(s, wq3):
+            turned = psum.tile([P, 2, 2, P], F32, name="turned%d" % s, tag="mm", bufs=3)
+            for b in range(2):
+                for u in range(2):
+                    nc.tensor.transpose(turned[:, b, u, :], hid_t[s][:, u, b, :].bitcast(F32), ident[:])
+            grouped = keep.tile([P, PACK * HALF], BF16, name="hid_bf%d" % s, align_bytes=64)
+            nc.scalar.copy(
+                out=grouped[:].bitcast(F32).rearrange("p (b j u) -> p b j u", b=2, u=2),
+                in_=turned[:].rearrange("p b u j -> p b j u"),
+            )
+            codes, scales = quantize(grouped, "hid%d" % s)
+            acc = psum.tile([P, 2, HALF], F32, name="acc%d" % s, tag="mm", bufs=3)
+            for m in range(2):
+                cols = slice(m * P, (m + 1) * P)
+                nc.tensor.matmul_mx(
+                    out=acc[:, m, :], lhsT=wq3[0][:, cols].bitcast(FP8X4), lhsT_scale=wq3[1][:, cols],
+                    rhs=codes[:].bitcast(FP8X4), rhs_scale=scales[:], start=True, stop=True,
+                )
+            result = keep.tile([P, 2, HALF], F32, name="result%d" % s)
+            nc.scalar.copy(out=result[:], in_=acc[:])
+            nc.sync.dma_start(
+                out=out[:, s * HALF : (s + 1) * HALF].rearrange("(m p) j -> p m j", m=2), in_=result[:]
+            )
+
+        wq1 = prepare_first(w1_raw[0], "w1a", nc.vector.tensor_copy)
+        wq2 = prepare_first(w2_raw[0], "w2a", nc.vector.tensor_copy)
+        channels(0, 0, wq1, wq2)
+        channels(0, 1, wq1, wq2)
+        banks00 = front(0, 0)
+        wq1 = prepare_first(w1_raw[1], "w1b", nc.vector.tensor_copy)
+        wq2 = prepare_first(w2_raw[1], "w2b", nc.vector.tensor_copy)
+        back(0, 0, banks00)
+        banks01 = front(0, 1)
+        channels(1, 0, wq1, wq2)
+        channels(1, 1, wq1, wq2)
+        back(0, 1, banks01)
+        banks10 = front(1, 0)
+        wq3 = prepare_last(w3_raw, "w3", nc.vector.tensor_copy)
+        back(1, 0, banks10)
+        banks11 = front(1, 1)
+        streams(0, wq3)
+        back(1, 1, banks11)
+        streams(1, wq3)

@@ -19,7 +19,7 @@ ACT = mybir.ActivationFunctionType
 P = 128
 PACK = 4
 HALF = 256
-LIST_COLS = HALF // 16
+CHUNKS = ((0, 256), (256, 128), (384, 128))
 
 
 def tile_picked_yalamo_lin_p_kernel(
@@ -48,27 +48,30 @@ def tile_picked_yalamo_lin_p_kernel(
             nc.sync.dma_start(out=rows[:], in_=r[h * HALF : (h + 1) * HALF, :].rearrange("(m u) c -> m u c", u=2))
             return rows
 
-        nc.vector.memset(table_scales[:].bitcast(I32), 0)
+        nc.gpsimd.memset(table_scales[:].bitcast(I32), 0)
+        w1_raw, w2_raw, ra_sb, rb_sb = {}, {}, {}, {}
         nc.sync.dma_start(offs_sb[:], offs)
-        nc.sync.dma_start(out=table_words[:], in_=x_words[0].rearrange("p n t -> p (n t)").bitcast(I32))
+        w1_raw[0] = load_weight(w1, 0, "w1_raw0")
         for q in range(4):
-            nc.scalar.dma_start(
+            nc.sync.dma_start(
                 out=table_scales[32 * q : 32 * q + 4, :].bitcast(I32),
                 in_=x_scales[0, 4 * q : 4 * q + 4, :].bitcast(I32),
             )
-        w1_raw, w2_raw, ra_sb, rb_sb = {}, {}, {}, {}
-        w1_raw[0] = load_weight(w1, 0, "w1_raw0")
+        nc.sync.dma_start(out=table_words[:], in_=x_words[0].rearrange("p n t -> p (n t)").bitcast(I32))
         w2_raw[0] = load_weight(w2, 0, "w2_raw0")
-        nc.sync.dma_start(ant_sb[:], ant)
         nc.sync.dma_start(out=unit_sb[:], in_=unit.rearrange("(h m u) o -> m h (u o)", h=2, u=2))
+        nc.sync.dma_start(ant_sb[:], ant)
         ra_sb[0] = load_received(ra, 0, "ra0")
-        rb_sb[0] = load_received(rb, 0, "rb0")
         w1_raw[1] = load_weight(w1, HALF, "w1_raw1")
+        rb_sb[0] = load_received(rb, 0, "rb0")
         w2_raw[1] = load_weight(w2, HALF, "w2_raw1")
         ra_sb[1] = load_received(ra, 1, "ra1")
         rb_sb[1] = load_received(rb, 1, "rb1")
         w3_raw = load_weight(w3, 0, "w3_raw")
         make_identity(nc, ident[:])
+
+        warm = keep.tile([P, 1], F32, name="warm")
+        nc.scalar.activation(warm[:], ident[:, 0:1], ACT.Abs_reciprocal_sqrt, bias=0.3)
 
         def quantize(grouped, name):
             width = grouped.shape[1] // PACK
@@ -98,8 +101,8 @@ def tile_picked_yalamo_lin_p_kernel(
         nc.vector.tensor_copy(x_bytes[:], table_scales[:].indirect(offs_sb[:]))
         nc.vector.tensor_copy(x_codes[:], table_words[:].bitcast(U32).indirect(offs_sb[:]))
 
-        factor = keep.tile([P, 3, 4], F32, name="factor")
-        for n, c in enumerate((0.5, 0.25, -0.25)):
+        factor = keep.tile([P, 2, 4], F32, name="factor")
+        for n, c in enumerate((0.5, 0.25)):
             nc.vector.tensor_scalar(
                 factor[:, n, :], unit_sb[:].rearrange("p h u -> p (h u)"), c, 0.0, ALU.mult, ALU.add
             )
@@ -109,7 +112,7 @@ def tile_picked_yalamo_lin_p_kernel(
 
         def product(w, u, name):
             codes, scales = w
-            bank = psum.tile([P, S], F32, name=name, tag="mm", bufs=3)
+            bank = psum.tile([P, S], F32, name=name, tag="mm", bufs=2)
             cols = slice(u * P, (u + 1) * P)
             nc.tensor.matmul_mx(
                 out=bank[:], lhsT=codes[:, cols].bitcast(FP8X4), lhsT_scale=scales[:, cols],
@@ -127,15 +130,17 @@ def tile_picked_yalamo_lin_p_kernel(
             hi = keep.tile([P, S], F32, name="hi" + name)
             hr_sq = keep.tile([P, S], F32, name="hr_sq" + name)
             hi_sq = keep.tile([P, S], F32, name="hi_sq" + name)
-            nc.scalar.copy(out=hr[:], in_=hr_ps[:])
-            nc.scalar.copy(out=hi[:], in_=hi_ps[:])
+            nc.scalar.activation(hr[:], hr_ps[:], ACT.Copy, scale=scalar_of(0, h, u))
             nc.scalar.activation(hr_sq[:], hr_ps[:], ACT.Square)
             nc.scalar.activation(hi_sq[:], hi_ps[:], ACT.Square)
+            nc.scalar.activation(hi[:], hi_ps[:], ACT.Copy, scale=scalar_of(1, h, u))
+            own = keep.tile([P, S], F32, name="own" + name)
             hr_ra = keep.tile([P, S], F32, name="hr_ra" + name)
             hi_rb = keep.tile([P, S], F32, name="hi_rb" + name)
-            nc.vector.scalar_tensor_tensor(hr_ra[:], hr[:], scalar_of(0, h, u), ra_sb[h][:, u, :], ALU.mult, ALU.mult)
-            nc.vector.scalar_tensor_tensor(hi_rb[:], hi[:], scalar_of(2, h, u), rb_sb[h][:, u, :], ALU.mult, ALU.mult)
-            rows[h, u] = (hr, hi, hr_sq, hi_sq, hr_ra, hi_rb)
+            nc.vector.tensor_tensor(own[:], hr_sq[:], hi_sq[:], ALU.add)
+            nc.vector.tensor_tensor(hr_ra[:], hr[:], ra_sb[h][:, u, :], ALU.mult)
+            nc.vector.scalar_tensor_tensor(hi_rb[:], hi[:], -1.0, rb_sb[h][:, u, :], ALU.mult, ALU.mult)
+            rows[h, u] = (hr, hi, own, hr_ra, hi_rb)
 
         def add_turned(bank, n, terms):
             for i, term in enumerate(terms):
@@ -144,98 +149,105 @@ def tile_picked_yalamo_lin_p_kernel(
                     is_transpose=True, start=(i == 0), stop=(i == len(terms) - 1),
                 )
 
-        def front(h, s):
-            cols = slice(s * HALF, (s + 1) * HALF)
-            places = ant_sb[:, s * LIST_COLS : (s + 1) * LIST_COLS]
-            name = "%d%d" % (h, s)
-            en = psum.tile([P, S], F32, name="en" + name, tag="en", bufs=1)
-            ta = psum.tile([P, S], F32, name="ta" + name, tag="ta", bufs=2)
-            tb = psum.tile([P, S], F32, name="tb" + name, tag="tb", bufs=2)
-            made = []
-            for u in range(2):
-                hr, hi = rows[h, u][0], rows[h, u][1]
-                got = work.tile([P, 2, HALF], F32, name="got", tag="got%d" % u)
-                got_sq = work.tile([P, 2, HALF], F32, name="got_sq", tag="got_sq%d" % u)
-                gr_rb = work.tile([P, HALF], F32, name="gr_rb", tag="gr_rb%d" % u)
-                gi_ra = work.tile([P, HALF], F32, name="gi_ra", tag="gi_ra%d" % u)
-                nc.vector.tensor_copy(got[:, 0, :], hr[:].indirect(places))
-                nc.scalar.activation(got[:, 1, :], hi[:].indirect(places), ACT.Copy)
-                nc.scalar.activation(got_sq[:], got[:], ACT.Square)
-                nc.vector.scalar_tensor_tensor(gr_rb[:], got[:, 0, :], scalar_of(0, h, u), rb_sb[h][:, u, cols], ALU.mult, ALU.mult)
-                nc.vector.scalar_tensor_tensor(gi_ra[:], got[:, 1, :], scalar_of(1, h, u), ra_sb[h][:, u, cols], ALU.mult, ALU.mult)
-                made.append((got_sq, gr_rb, gi_ra))
-            blocks = [(u, b) for u in range(2) for b in range(2)]
-            for n, (u, b) in enumerate(blocks):
-                near = slice(b * P, (b + 1) * P)
-                far = slice(s * HALF + b * P, s * HALF + (b + 1) * P)
-                add_turned(en, n, [rows[h, u][2][:, far], rows[h, u][3][:, far], made[u][0][:, 0, near], made[u][0][:, 1, near]])
-            for n, (u, b) in enumerate(blocks):
-                near = slice(b * P, (b + 1) * P)
-                far = slice(s * HALF + b * P, s * HALF + (b + 1) * P)
-                add_turned(tb, n, [rows[h, u][5][:, far], made[u][2][:, near]])
-            for n, (u, b) in enumerate(blocks):
-                near = slice(b * P, (b + 1) * P)
-                far = slice(s * HALF + b * P, s * HALF + (b + 1) * P)
-                add_turned(ta, n, [rows[h, u][4][:, far], made[u][1][:, near], made[u][2][:, near]])
+        def front(h, pieces, plain=False):
+            total = sum(width for u, j0, width in pieces)
+            name = "%d_%d_%d" % (h, pieces[0][0], pieces[0][1])
+            en = psum.tile([P, total], F32, name="en" + name, tag="en", bufs=2)
+            ta = psum.tile([P, total], F32, name="ta" + name, tag="ta", bufs=2)
+            tb = psum.tile([P, total], F32, name="tb" + name, tag="tb", bufs=2)
+            blocks = []
+            for n, (u, j0, width) in enumerate(pieces):
+                cols = slice(j0, j0 + width)
+                places = ant_sb[:, j0 // 16 : (j0 + width) // 16]
+                hr, hi, own, hr_ra, hi_rb = rows[h, u]
+                other = work.tile([P, width], F32, name="other", tag="other%d" % n)
+                gr_rb = work.tile([P, width], F32, name="gr_rb", tag="gr_rb%d" % n)
+                gi_ra = work.tile([P, width], F32, name="gi_ra", tag="gi_ra%d" % n)
+                nc.scalar.activation(other[:], own[:].indirect(places), ACT.Copy)
+                if plain:
+                    gi = work.tile([P, width], F32, name="gi", tag="gi%d" % n)
+                    nc.scalar.activation(gi[:], hi[:].indirect(places), ACT.Copy)
+                    nc.vector.tensor_tensor(gi_ra[:], gi[:], ra_sb[h][:, u, cols], ALU.mult)
+                else:
+                    nc.vector.tensor_tensor(gi_ra[:], hi[:].indirect(places), ra_sb[h][:, u, cols], ALU.mult)
+                nc.vector.tensor_tensor(gr_rb[:], hr[:].indirect(places), rb_sb[h][:, u, cols], ALU.mult)
+                for b in range(0, width, P):
+                    near, far = slice(b, b + P), slice(j0 + b, j0 + b + P)
+                    blocks.append(([other[:, near], own[:, far]], [gi_ra[:, near], hi_rb[:, far]], [gr_rb[:, near], gi_ra[:, near], hr_ra[:, far]]))
+            for k, bank in enumerate((en, tb, ta)):
+                for n, terms in enumerate(blocks):
+                    add_turned(bank, n, terms[k])
             return en, ta, tb
 
-        hid_t = [keep.tile([P, 2, 2, HALF], BF16, name="hid_t%d" % s) for s in range(2)]
+        hid_t = {j0: keep.tile([P, 2, width // P, HALF], BF16, name="hid_t%d" % j0) for j0, width in CHUNKS}
 
-        def back(h, s, banks):
+        def back(h, pieces, banks):
             en, ta, tb = banks
-            root = work.tile([P, S], F32, name="root")
-            part = work.tile([P, S], F32, name="part")
-            both = work.tile([P, S], F32, name="both")
+            total = sum(width for u, j0, width in pieces)
+            root = work.tile([P, total], F32, name="root")
+            part = work.tile([P, total], F32, name="part")
+            both = work.tile([P, total], F32, name="both")
             nc.scalar.activation(root[:], en[:], ACT.Abs_reciprocal_sqrt, bias=0.3)
             nc.vector.scalar_tensor_tensor(part[:], root[:], -0.25, tb[:], ALU.add, ALU.mult)
             nc.vector.scalar_tensor_tensor(both[:], part[:], 4.0, ta[:], ALU.mult, ALU.add)
-            nc.vector.tensor_tensor(
-                hid_t[s][:, :, :, h * P : (h + 1) * P],
-                both[:].rearrange("p (u b m) -> p u b m", u=2, b=2),
-                root[:].rearrange("p (u b m) -> p u b m", u=2, b=2),
-                ALU.mult,
-            )
+            tiles = sorted(set(u for u, j0, width in pieces))
+            first = pieces[0][1]
+            for c0, cw in CHUNKS:
+                if first <= c0 < first + total // len(tiles):
+                    blocks = slice((c0 - first) // P, (c0 - first + cw) // P)
+                    nc.vector.tensor_tensor(
+                        hid_t[c0][:, tiles[0] : tiles[-1] + 1, :, h * P : (h + 1) * P],
+                        both[:].rearrange("p (u b m) -> p u b m", u=len(tiles), m=P)[:, :, blocks, :],
+                        root[:].rearrange("p (u b m) -> p u b m", u=len(tiles), m=P)[:, :, blocks, :],
+                        ALU.mult,
+                    )
 
-        def streams(s, wq3):
-            turned = psum.tile([P, 2, 2, P], F32, name="turned%d" % s, tag="mm", bufs=3)
-            for b in range(2):
+        def streams(j0, width, wq3):
+            turned = psum.tile([P, width // P, 2, P], F32, name="turned%d" % j0, tag="mm", bufs=2)
+            for b in range(width // P):
                 for u in range(2):
-                    nc.tensor.transpose(turned[:, b, u, :], hid_t[s][:, u, b, :].bitcast(F32), ident[:])
-            grouped = keep.tile([P, PACK * HALF], BF16, name="hid_bf%d" % s, align_bytes=64)
+                    nc.tensor.transpose(turned[:, b, u, :], hid_t[j0][:, u, b, :].bitcast(F32), ident[:])
+            grouped = keep.tile([P, PACK * width], BF16, name="hid_bf%d" % j0, align_bytes=64)
             nc.scalar.copy(
-                out=grouped[:].bitcast(F32).rearrange("p (b j u) -> p b j u", b=2, u=2),
+                out=grouped[:].bitcast(F32).rearrange("p (b j u) -> p b j u", j=P, u=2),
                 in_=turned[:].rearrange("p b u j -> p b j u"),
             )
-            codes, scales = quantize(grouped, "hid%d" % s)
-            acc = psum.tile([P, 2, HALF], F32, name="acc%d" % s, tag="mm", bufs=3)
+            codes, scales = quantize(grouped, "hid%d" % j0)
+            acc = psum.tile([P, 2, width], F32, name="acc%d" % j0, tag="mm", bufs=2)
             for m in range(2):
                 cols = slice(m * P, (m + 1) * P)
                 nc.tensor.matmul_mx(
                     out=acc[:, m, :], lhsT=wq3[0][:, cols].bitcast(FP8X4), lhsT_scale=wq3[1][:, cols],
                     rhs=codes[:].bitcast(FP8X4), rhs_scale=scales[:], start=True, stop=True,
                 )
-            result = keep.tile([P, 2, HALF], F32, name="result%d" % s)
-            nc.scalar.copy(out=result[:], in_=acc[:])
-            nc.sync.dma_start(
-                out=out[:, s * HALF : (s + 1) * HALF].rearrange("(m p) j -> p m j", m=2), in_=result[:]
-            )
+            result = keep.tile([P, 2, width], F32, name="result%d" % j0)
+            nc.vector.tensor_copy(out=result[:], in_=acc[:])
+            nc.sync.dma_start(out=out[:, j0 : j0 + width].rearrange("(m p) j -> p m j", m=2), in_=result[:])
 
         wq1 = prepare_first(w1_raw[0], "w1a", nc.vector.tensor_copy)
         wq2 = prepare_first(w2_raw[0], "w2a", nc.vector.tensor_copy)
         channels(0, 0, wq1, wq2)
+        t0 = [(0, 0, HALF), (0, HALF, HALF)]
+        bt0 = front(0, t0, False)
         channels(0, 1, wq1, wq2)
-        banks00 = front(0, 0)
-        wq1 = prepare_first(w1_raw[1], "w1b", nc.vector.tensor_copy)
-        wq2 = prepare_first(w2_raw[1], "w2b", nc.vector.tensor_copy)
-        back(0, 0, banks00)
-        banks01 = front(0, 1)
-        channels(1, 0, wq1, wq2)
-        channels(1, 1, wq1, wq2)
-        back(0, 1, banks01)
-        banks10 = front(1, 0)
-        wq3 = prepare_last(w3_raw, "w3", nc.vector.tensor_copy)
-        back(1, 0, banks10)
-        banks11 = front(1, 1)
-        streams(0, wq3)
-        back(1, 1, banks11)
-        streams(1, wq3)
+        wq1b = prepare_first(w1_raw[1], "w1b", nc.scalar.copy)
+        wq2b = prepare_first(w2_raw[1], "w2b", nc.scalar.copy)
+        wq3 = prepare_last(w3_raw, "w3", nc.scalar.copy)
+        back(0, t0, bt0)
+        channels(1, 0, wq1b, wq2b)
+        t1 = [(1, 0, HALF), (1, HALF, HALF)]
+        bt1 = front(0, t1, False)
+        channels(1, 1, wq1b, wq2b)
+        back(0, t1, bt1)
+        p0 = [(u, CHUNKS[0][0], CHUNKS[0][1]) for u in range(2)]
+        b0 = front(1, p0, False)
+        back(1, p0, b0)
+        p1 = [(u, CHUNKS[1][0], CHUNKS[1][1]) for u in range(2)]
+        b1 = front(1, p1, False)
+        streams(CHUNKS[0][0], CHUNKS[0][1], wq3)
+        back(1, p1, b1)
+        p2 = [(u, CHUNKS[2][0], CHUNKS[2][1]) for u in range(2)]
+        b2 = front(1, p2, False)
+        streams(CHUNKS[1][0], CHUNKS[1][1], wq3)
+        back(1, p2, b2)
+        streams(CHUNKS[2][0], CHUNKS[2][1], wq3)

@@ -4,7 +4,7 @@ import concourse.mybir as mybir
 from concourse.masks import make_identity
 
 K, T, S, N, H = 512, 2048, 512, 256, 512
-FLOPS = 2 * K * H * S * 2 + 2 * H * N * S
+FLOPS = 2 * (2 * K * H * S) + 2 * H * N * S
 
 F32 = mybir.dt.float32
 BF16 = mybir.dt.bfloat16
@@ -18,8 +18,11 @@ ACT = mybir.ActivationFunctionType
 
 P = 128
 PACK = 4
-HALF = 256
-CHUNKS = ((0, 256), (256, 128), (384, 128))
+TILES = H // P
+GATHER = 256
+LIST_ROWS = 16
+LOADS = [[0],[1],[2,3]]
+STRETCHES = ((0, 256), (256, 128), (384, 128))
 
 
 def tile_picked_yalamo_lin_p_kernel(
@@ -29,47 +32,53 @@ def tile_picked_yalamo_lin_p_kernel(
     with ExitStack() as ctx:
         keep = ctx.enter_context(tc.tile_pool(name="keep", bufs=1))
         work = ctx.enter_context(tc.tile_pool(name="work", bufs=2))
-        psum = ctx.enter_context(tc.psum_pool(name="psum", bufs=1))
+        psum = ctx.enter_context(tc.psum_pool(name="psum", bufs=2))
 
-        offs_sb = keep.tile([P, S // 16], U16, name="offs_sb")
-        ant_sb = keep.tile([P, S // 16], U16, name="ant_sb")
+        offs_sb = keep.tile([P, S // LIST_ROWS], U16, name="offs_sb")
+        ant_sb = keep.tile([P, S // LIST_ROWS], U16, name="ant_sb")
         table_words = keep.tile([P, T], I32, name="table_words", align_bytes=64)
         table_scales = keep.tile([P, T], U8, name="table_scales", align_bytes=64)
-        unit_sb = keep.tile([P, 2, 2], F32, name="unit_sb")
+        unit_sb = keep.tile([P, TILES], F32, name="unit_sb")
         ident = keep.tile([P, P], F32, name="ident")
 
-        def load_weight(w, c0, name):
-            raw = keep.tile([P, PACK, HALF], F32, name=name)
-            nc.sync.dma_start(out=raw[:], in_=w[:, c0 : c0 + HALF].rearrange("(p j) c -> p j c", j=PACK))
+        def load_weight(w, first, count, name):
+            raw = keep.tile([P, PACK, count], F32, name=name)
+            nc.sync.dma_start(out=raw[:], in_=w[:, first : first + count].rearrange("(p j) c -> p j c", j=PACK))
             return raw
 
-        def load_received(r, h, name):
-            rows = keep.tile([P, 2, S], F32, name=name)
-            nc.sync.dma_start(out=rows[:], in_=r[h * HALF : (h + 1) * HALF, :].rearrange("(m u) c -> m u c", u=2))
-            return rows
+        def load_received(r, tiles, name):
+            rows = keep.tile([P, len(tiles), S], F32, name=name)
+            nc.sync.dma_start(
+                out=rows[:], in_=r[tiles[0] * P : (tiles[-1] + 1) * P, :].rearrange("(b p) c -> p b c", p=P)
+            )
+            return {b: rows[:, n, :] for n, b in enumerate(tiles)}
 
         nc.gpsimd.memset(table_scales[:].bitcast(I32), 0)
         w1_raw, w2_raw, ra_sb, rb_sb = {}, {}, {}, {}
         nc.sync.dma_start(offs_sb[:], offs)
-        w1_raw[0] = load_weight(w1, 0, "w1_raw0")
+        w1_raw[0] = load_weight(w1, 0, 128, "w1_raw0")
+        w2_raw[0] = load_weight(w2, 0, 128, "w2_raw0")
         for q in range(4):
             nc.sync.dma_start(
                 out=table_scales[32 * q : 32 * q + 4, :].bitcast(I32),
                 in_=x_scales[0, 4 * q : 4 * q + 4, :].bitcast(I32),
             )
         nc.sync.dma_start(out=table_words[:], in_=x_words[0].rearrange("p n t -> p (n t)").bitcast(I32))
-        w2_raw[0] = load_weight(w2, 0, "w2_raw0")
-        nc.sync.dma_start(out=unit_sb[:], in_=unit.rearrange("(h m u) o -> m h (u o)", h=2, u=2))
+        with nc.allow_non_contiguous_dma(reason="one value a partition and tile"):
+            nc.sync.dma_start(out=unit_sb[:], in_=unit.rearrange("(b p) o -> p (b o)", p=P))
         nc.sync.dma_start(ant_sb[:], ant)
-        ra_sb[0] = load_received(ra, 0, "ra0")
-        w1_raw[1] = load_weight(w1, HALF, "w1_raw1")
-        rb_sb[0] = load_received(rb, 0, "rb0")
-        w2_raw[1] = load_weight(w2, HALF, "w2_raw1")
-        ra_sb[1] = load_received(ra, 1, "ra1")
-        rb_sb[1] = load_received(rb, 1, "rb1")
-        w3_raw = load_weight(w3, 0, "w3_raw")
+        w1_raw[1] = load_weight(w1, 128, 128, "w1_raw1")
+        w2_raw[1] = load_weight(w2, 128, 128, "w2_raw1")
+        ra_sb.update(load_received(ra, (0,), "ra0"))
+        rb_sb.update(load_received(rb, (0,), "rb0"))
+        w1_raw[2] = load_weight(w1, 256, 256, "w1_raw2")
+        w2_raw[2] = load_weight(w2, 256, 256, "w2_raw2")
+        ra_sb.update(load_received(ra, (1,), "ra1"))
+        rb_sb.update(load_received(rb, (1,), "rb1"))
+        ra_sb.update(load_received(ra, (2, 3,), "ra23"))
+        rb_sb.update(load_received(rb, (2, 3,), "rb23"))
+        w3_raw = load_weight(w3, 0, N, "w3_raw")
         make_identity(nc, ident[:])
-
         warm = keep.tile([P, 1], F32, name="warm")
         nc.scalar.activation(warm[:], ident[:, 0:1], ACT.Abs_reciprocal_sqrt, bias=0.3)
 
@@ -80,174 +89,154 @@ def tile_picked_yalamo_lin_p_kernel(
             nc.vector.quantize_mx(out=codes[:].bitcast(FP8X4), scales=scales[:], in_=grouped[:])
             return codes, scales
 
-        def prepare_first(raw, name, copy):
-            grouped = keep.tile([P, PACK * HALF], BF16, name=name + "_bf", align_bytes=64)
+        def quantize_weight(raw, name, copy):
+            grouped = keep.tile([P, PACK * raw.shape[2]], BF16, name=name + "_bf", align_bytes=64)
             copy(
-                out=grouped[:].rearrange("p (u a l j) -> p a j l u", u=2, l=2, j=PACK),
-                in_=raw[:].rearrange("p j (a l u) -> p a j l u", l=2, u=2),
+                out=grouped[:].rearrange("p (a i j) -> p a j i", i=4, j=PACK),
+                in_=raw[:].rearrange("p j (a i) -> p a j i", i=4),
             )
             return quantize(grouped, name)
 
-        def prepare_last(raw, name, copy):
-            grouped = keep.tile([P, PACK * N], BF16, name=name + "_bf", align_bytes=64)
-            copy(
-                out=grouped[:].rearrange("p (a i u e) -> p a e u i", i=4, u=2, e=2),
-                in_=raw[:].rearrange("p (e u) (a i) -> p a e u i", u=2, i=4),
+        def multiply(bank, weight, first, codes, scales):
+            cols = slice(first, first + P)
+            nc.tensor.matmul_mx(
+                out=bank, lhsT=weight[0][:, cols].bitcast(FP8X4), lhsT_scale=weight[1][:, cols],
+                rhs=codes[:].bitcast(FP8X4), rhs_scale=scales[:], start=True, stop=True,
             )
-            return quantize(grouped, name)
 
         x_codes = keep.tile([P, S], U32, name="x_codes", align_bytes=64)
         x_bytes = keep.tile([P, S], U8, name="x_bytes", align_bytes=64)
         nc.vector.tensor_copy(x_bytes[:], table_scales[:].indirect(offs_sb[:]))
         nc.vector.tensor_copy(x_codes[:], table_words[:].bitcast(U32).indirect(offs_sb[:]))
 
-        factor = keep.tile([P, 2, 4], F32, name="factor")
-        for n, c in enumerate((0.5, 0.25)):
-            nc.vector.tensor_scalar(
-                factor[:, n, :], unit_sb[:].rearrange("p h u -> p (h u)"), c, 0.0, ALU.mult, ALU.add
-            )
-
-        def scalar_of(n, h, u):
-            return factor[:, n, 2 * h + u : 2 * h + u + 1]
-
-        def product(w, u, name):
-            codes, scales = w
-            bank = psum.tile([P, S], F32, name=name, tag="mm", bufs=2)
-            cols = slice(u * P, (u + 1) * P)
-            nc.tensor.matmul_mx(
-                out=bank[:], lhsT=codes[:, cols].bitcast(FP8X4), lhsT_scale=scales[:, cols],
-                rhs=x_codes[:].bitcast(FP8X4), rhs_scale=x_bytes[:], start=True, stop=True,
-            )
-            return bank
+        unit_half = keep.tile([P, TILES], F32, name="unit_half")
+        unit_quarter = keep.tile([P, TILES], F32, name="unit_quarter")
+        nc.vector.tensor_scalar(unit_half[:], unit_sb[:], 0.5, 0.0, ALU.mult, ALU.add)
+        nc.vector.tensor_scalar(unit_quarter[:], unit_sb[:], 0.25, 0.0, ALU.mult, ALU.add)
 
         rows = {}
 
-        def channels(h, u, wq1, wq2):
-            name = "%d%d" % (h, u)
-            hr_ps = product(wq1, u, "hr_ps" + name)
-            hi_ps = product(wq2, u, "hi_ps" + name)
-            hr = keep.tile([P, S], F32, name="hr" + name)
-            hi = keep.tile([P, S], F32, name="hi" + name)
-            hr_sq = keep.tile([P, S], F32, name="hr_sq" + name)
-            hi_sq = keep.tile([P, S], F32, name="hi_sq" + name)
-            nc.scalar.activation(hr[:], hr_ps[:], ACT.Copy, scale=scalar_of(0, h, u))
+        def channels(b, wq1, wq2, first):
+            hr_ps = psum.tile([P, S], F32, name="hr_ps", tag="product")
+            hi_ps = psum.tile([P, S], F32, name="hi_ps", tag="product")
+            multiply(hr_ps[:], wq1, first, x_codes, x_bytes)
+            multiply(hi_ps[:], wq2, first, x_codes, x_bytes)
+            hr = keep.tile([P, S], F32, name="hr%d" % b)
+            hi = keep.tile([P, S], F32, name="hi%d" % b)
+            hr_sq = work.tile([P, S], F32, name="hr_sq")
+            hi_sq = work.tile([P, S], F32, name="hi_sq")
+            nc.scalar.activation(hr[:], hr_ps[:], ACT.Copy, scale=unit_half[:, b : b + 1])
             nc.scalar.activation(hr_sq[:], hr_ps[:], ACT.Square)
             nc.scalar.activation(hi_sq[:], hi_ps[:], ACT.Square)
-            nc.scalar.activation(hi[:], hi_ps[:], ACT.Copy, scale=scalar_of(1, h, u))
-            own = keep.tile([P, S], F32, name="own" + name)
-            hr_ra = keep.tile([P, S], F32, name="hr_ra" + name)
-            hi_rb = keep.tile([P, S], F32, name="hi_rb" + name)
+            nc.scalar.activation(hi[:], hi_ps[:], ACT.Copy, scale=unit_quarter[:, b : b + 1])
+            own = keep.tile([P, S], F32, name="own%d" % b)
+            hr_ra = keep.tile([P, S], F32, name="hr_ra%d" % b)
+            hi_rb = keep.tile([P, S], F32, name="hi_rb%d" % b)
             nc.vector.tensor_tensor(own[:], hr_sq[:], hi_sq[:], ALU.add)
-            nc.vector.tensor_tensor(hr_ra[:], hr[:], ra_sb[h][:, u, :], ALU.mult)
-            nc.vector.scalar_tensor_tensor(hi_rb[:], hi[:], -1.0, rb_sb[h][:, u, :], ALU.mult, ALU.mult)
-            rows[h, u] = (hr, hi, own, hr_ra, hi_rb)
+            nc.vector.tensor_tensor(hr_ra[:], hr[:], ra_sb[b], ALU.mult)
+            nc.vector.scalar_tensor_tensor(hi_rb[:], hi[:], -1.0, rb_sb[b], ALU.mult, ALU.mult)
+            return hr, hi, own, hr_ra, hi_rb
 
-        def add_turned(bank, n, terms):
-            for i, term in enumerate(terms):
-                nc.tensor.matmul(
-                    out=bank[:, n * P : (n + 1) * P], lhsT=term, rhs=ident[:],
-                    is_transpose=True, start=(i == 0), stop=(i == len(terms) - 1),
-                )
-
-        def front(h, pieces, plain=False):
-            total = sum(width for u, j0, width in pieces)
-            name = "%d_%d_%d" % (h, pieces[0][0], pieces[0][1])
-            en = psum.tile([P, total], F32, name="en" + name, tag="en", bufs=2)
-            ta = psum.tile([P, total], F32, name="ta" + name, tag="ta", bufs=2)
-            tb = psum.tile([P, total], F32, name="tb" + name, tag="tb", bufs=2)
-            blocks = []
-            for n, (u, j0, width) in enumerate(pieces):
+        def sums(tiles, first, count, scalar_fetches):
+            en = psum.tile([P, len(tiles) * count], F32, name="en", tag="energy")
+            ta = psum.tile([P, len(tiles) * count], F32, name="ta", tag="ta")
+            tb = psum.tile([P, len(tiles) * count], F32, name="tb", tag="tb")
+            terms = {}
+            pieces = [(b, j0) for b in tiles for j0 in range(first, first + count, GATHER)]
+            for n, (b, j0) in enumerate(pieces):
+                hr, hi, own, hr_ra, hi_rb = rows[b]
+                width = min(GATHER, first + count - j0)
                 cols = slice(j0, j0 + width)
-                places = ant_sb[:, j0 // 16 : (j0 + width) // 16]
-                hr, hi, own, hr_ra, hi_rb = rows[h, u]
+                places = ant_sb[:, j0 // LIST_ROWS : (j0 + width) // LIST_ROWS]
                 other = work.tile([P, width], F32, name="other", tag="other%d" % n)
                 gr_rb = work.tile([P, width], F32, name="gr_rb", tag="gr_rb%d" % n)
                 gi_ra = work.tile([P, width], F32, name="gi_ra", tag="gi_ra%d" % n)
                 nc.scalar.activation(other[:], own[:].indirect(places), ACT.Copy)
-                if plain:
+                if scalar_fetches:
                     gi = work.tile([P, width], F32, name="gi", tag="gi%d" % n)
                     nc.scalar.activation(gi[:], hi[:].indirect(places), ACT.Copy)
-                    nc.vector.tensor_tensor(gi_ra[:], gi[:], ra_sb[h][:, u, cols], ALU.mult)
+                    nc.vector.tensor_tensor(gi_ra[:], gi[:], ra_sb[b][:, cols], ALU.mult)
                 else:
-                    nc.vector.tensor_tensor(gi_ra[:], hi[:].indirect(places), ra_sb[h][:, u, cols], ALU.mult)
-                nc.vector.tensor_tensor(gr_rb[:], hr[:].indirect(places), rb_sb[h][:, u, cols], ALU.mult)
-                for b in range(0, width, P):
-                    near, far = slice(b, b + P), slice(j0 + b, j0 + b + P)
-                    blocks.append(([other[:, near], own[:, far]], [gi_ra[:, near], hi_rb[:, far]], [gr_rb[:, near], gi_ra[:, near], hr_ra[:, far]]))
+                    nc.vector.tensor_tensor(gi_ra[:], hi[:].indirect(places), ra_sb[b][:, cols], ALU.mult)
+                nc.vector.tensor_tensor(gr_rb[:], hr[:].indirect(places), rb_sb[b][:, cols], ALU.mult)
+                for c in range(0, width, P):
+                    near, far = slice(c, c + P), slice(j0 + c, j0 + c + P)
+                    place = (j0 + c - first) // P * len(tiles) + tiles.index(b)
+                    terms[place] = (
+                        [other[:, near], own[:, far]],
+                        [gi_ra[:, near], hi_rb[:, far]],
+                        [gr_rb[:, near], gi_ra[:, near], hr_ra[:, far]],
+                    )
             for k, bank in enumerate((en, tb, ta)):
-                for n, terms in enumerate(blocks):
-                    add_turned(bank, n, terms[k])
+                for place, block in terms.items():
+                    for i, term in enumerate(block[k]):
+                        nc.tensor.matmul(
+                            out=bank[:, place * P : (place + 1) * P], lhsT=term, rhs=ident[:],
+                            is_transpose=True, start=(i == 0), stop=(i == len(block[k]) - 1),
+                        )
             return en, ta, tb
 
-        hid_t = {j0: keep.tile([P, 2, width // P, HALF], BF16, name="hid_t%d" % j0) for j0, width in CHUNKS}
+        hid_turned = {j0: keep.tile([P, count // P, H], BF16, name="hid_turned%d" % j0) for j0, count in STRETCHES}
 
-        def back(h, pieces, banks):
+        def combine(tiles, first, count, banks):
             en, ta, tb = banks
-            total = sum(width for u, j0, width in pieces)
-            root = work.tile([P, total], F32, name="root")
-            part = work.tile([P, total], F32, name="part")
-            both = work.tile([P, total], F32, name="both")
+            features = len(tiles) * P
+            root = work.tile([P, len(tiles) * count], F32, name="root")
+            part = work.tile([P, len(tiles) * count], F32, name="part")
+            both = work.tile([P, len(tiles) * count], F32, name="both")
             nc.scalar.activation(root[:], en[:], ACT.Abs_reciprocal_sqrt, bias=0.3)
             nc.vector.scalar_tensor_tensor(part[:], root[:], -0.25, tb[:], ALU.add, ALU.mult)
             nc.vector.scalar_tensor_tensor(both[:], part[:], 4.0, ta[:], ALU.mult, ALU.add)
-            tiles = sorted(set(u for u, j0, width in pieces))
-            first = pieces[0][1]
-            for c0, cw in CHUNKS:
-                if first <= c0 < first + total // len(tiles):
-                    blocks = slice((c0 - first) // P, (c0 - first + cw) // P)
+            for j0, width in STRETCHES:
+                if first <= j0 < first + count:
+                    blocks = slice((j0 - first) // P, (j0 - first + width) // P)
                     nc.vector.tensor_tensor(
-                        hid_t[c0][:, tiles[0] : tiles[-1] + 1, :, h * P : (h + 1) * P],
-                        both[:].rearrange("p (u b m) -> p u b m", u=len(tiles), m=P)[:, :, blocks, :],
-                        root[:].rearrange("p (u b m) -> p u b m", u=len(tiles), m=P)[:, :, blocks, :],
+                        hid_turned[j0][:, :, tiles[0] * P : tiles[0] * P + features],
+                        both[:].rearrange("p (n m) -> p n m", m=features)[:, blocks, :],
+                        root[:].rearrange("p (n m) -> p n m", m=features)[:, blocks, :],
                         ALU.mult,
                     )
 
-        def streams(j0, width, wq3):
-            turned = psum.tile([P, width // P, 2, P], F32, name="turned%d" % j0, tag="mm", bufs=2)
-            for b in range(width // P):
+        def streams(first, count, wq3):
+            back = psum.tile([P, count // P, 2, P], F32, name="back", tag="product")
+            for n in range(count // P):
+                words = hid_turned[first][:, n, :].bitcast(F32)
                 for u in range(2):
-                    nc.tensor.transpose(turned[:, b, u, :], hid_t[j0][:, u, b, :].bitcast(F32), ident[:])
-            grouped = keep.tile([P, PACK * width], BF16, name="hid_bf%d" % j0, align_bytes=64)
+                    nc.tensor.transpose(back[:, n, u, :], words[:, u : H // 2 : 2], ident[:])
+            grouped = keep.tile([P, PACK * count], BF16, name="hid_bf%d" % first, align_bytes=64)
             nc.scalar.copy(
-                out=grouped[:].bitcast(F32).rearrange("p (b j u) -> p b j u", j=P, u=2),
-                in_=turned[:].rearrange("p b u j -> p b j u"),
+                out=grouped[:].bitcast(F32).rearrange("p (n j u) -> p n j u", j=P, u=2),
+                in_=back[:].rearrange("p n u j -> p n j u"),
             )
-            codes, scales = quantize(grouped, "hid%d" % j0)
-            acc = psum.tile([P, 2, width], F32, name="acc%d" % j0, tag="mm", bufs=2)
-            for m in range(2):
-                cols = slice(m * P, (m + 1) * P)
-                nc.tensor.matmul_mx(
-                    out=acc[:, m, :], lhsT=wq3[0][:, cols].bitcast(FP8X4), lhsT_scale=wq3[1][:, cols],
-                    rhs=codes[:].bitcast(FP8X4), rhs_scale=scales[:], start=True, stop=True,
-                )
-            result = keep.tile([P, 2, width], F32, name="result%d" % j0)
+            codes, scales = quantize(grouped, "hid%d" % first)
+            acc = psum.tile([P, N // P, count], F32, name="acc", tag="product")
+            for m in range(N // P):
+                multiply(acc[:, m, :], wq3, m * P, codes, scales)
+            result = keep.tile([P, N // P, count], F32, name="result%d" % first)
             nc.vector.tensor_copy(out=result[:], in_=acc[:])
-            nc.sync.dma_start(out=out[:, j0 : j0 + width].rearrange("(m p) j -> p m j", m=2), in_=result[:])
+            nc.sync.dma_start(out=out[:, first : first + count].rearrange("(m p) j -> p m j", p=P), in_=result[:])
 
-        wq1 = prepare_first(w1_raw[0], "w1a", nc.vector.tensor_copy)
-        wq2 = prepare_first(w2_raw[0], "w2a", nc.vector.tensor_copy)
-        channels(0, 0, wq1, wq2)
-        t0 = [(0, 0, HALF), (0, HALF, HALF)]
-        bt0 = front(0, t0, False)
-        channels(0, 1, wq1, wq2)
-        wq1b = prepare_first(w1_raw[1], "w1b", nc.scalar.copy)
-        wq2b = prepare_first(w2_raw[1], "w2b", nc.scalar.copy)
-        wq3 = prepare_last(w3_raw, "w3", nc.scalar.copy)
-        back(0, t0, bt0)
-        channels(1, 0, wq1b, wq2b)
-        t1 = [(1, 0, HALF), (1, HALF, HALF)]
-        bt1 = front(0, t1, False)
-        channels(1, 1, wq1b, wq2b)
-        back(0, t1, bt1)
-        p0 = [(u, CHUNKS[0][0], CHUNKS[0][1]) for u in range(2)]
-        b0 = front(1, p0, False)
-        back(1, p0, b0)
-        p1 = [(u, CHUNKS[1][0], CHUNKS[1][1]) for u in range(2)]
-        b1 = front(1, p1, False)
-        streams(CHUNKS[0][0], CHUNKS[0][1], wq3)
-        back(1, p1, b1)
-        p2 = [(u, CHUNKS[2][0], CHUNKS[2][1]) for u in range(2)]
-        b2 = front(1, p2, False)
-        streams(CHUNKS[1][0], CHUNKS[1][1], wq3)
-        back(1, p2, b2)
-        streams(CHUNKS[2][0], CHUNKS[2][1], wq3)
+        wq1_0 = quantize_weight(w1_raw[0], "w1_0", nc.vector.tensor_copy)
+        wq2_0 = quantize_weight(w2_raw[0], "w2_0", nc.vector.tensor_copy)
+        wq1_1 = quantize_weight(w1_raw[1], "w1_1", nc.vector.tensor_copy)
+        wq2_1 = quantize_weight(w2_raw[1], "w2_1", nc.vector.tensor_copy)
+        rows[0] = channels(0, wq1_0, wq2_0, 0)
+        m0_0 = sums([0], 0, S, False)
+        rows[1] = channels(1, wq1_1, wq2_1, 0)
+        wq1_2 = quantize_weight(w1_raw[2], "w1_2", nc.scalar.copy)
+        wq2_2 = quantize_weight(w2_raw[2], "w2_2", nc.scalar.copy)
+        wq3 = quantize_weight(w3_raw, "w3", nc.scalar.copy)
+        combine([0], 0, S, m0_0)
+        rows[2] = channels(2, wq1_2, wq2_2, 0)
+        m1_0 = sums([1], 0, S, False)
+        rows[3] = channels(3, wq1_2, wq2_2, 128)
+        combine([1], 0, S, m1_0)
+        m23_0 = sums([2, 3], 0, 256, False)
+        combine([2, 3], 0, 256, m23_0)
+        m23_256 = sums([2, 3], 256, 128, False)
+        streams(STRETCHES[0][0], STRETCHES[0][1], wq3)
+        combine([2, 3], 256, 128, m23_256)
+        m23_384 = sums([2, 3], 384, 128, False)
+        streams(STRETCHES[1][0], STRETCHES[1][1], wq3)
+        combine([2, 3], 384, 128, m23_384)
+        streams(STRETCHES[2][0], STRETCHES[2][1], wq3)

from contextlib import ExitStack

import concourse.mybir as mybir
from concourse.masks import make_identity

K, T, S, N, H = 512, 2048, 512, 256, 512
FLOPS = 2 * (2 * K * H * S) + 2 * H * N * S

F32 = mybir.dt.float32
BF16 = mybir.dt.bfloat16
I32 = mybir.dt.int32
U32 = mybir.dt.uint32
U16 = mybir.dt.uint16
U8 = mybir.dt.uint8
FP8X4 = mybir.dt.float8_e4m3fn_x4
ALU = mybir.AluOpType
ACT = mybir.ActivationFunctionType

P = 128
PACK = 4
TILES = H // P
GATHER = 256
LIST_ROWS = 16
LOADS = [[0],[1],[2,3]]
STRETCHES = ((0, 256), (256, 128), (384, 128))


def tile_picked_yalamo_lin_p_kernel(
    tc, x_words, x_scales, w1, w2, ra, rb, unit, w3, offs, ant, out
):
    nc = tc.nc
    with ExitStack() as ctx:
        keep = ctx.enter_context(tc.tile_pool(name="keep", bufs=1))
        work = ctx.enter_context(tc.tile_pool(name="work", bufs=2))
        psum = ctx.enter_context(tc.psum_pool(name="psum", bufs=2))

        offs_sb = keep.tile([P, S // LIST_ROWS], U16, name="offs_sb")
        ant_sb = keep.tile([P, S // LIST_ROWS], U16, name="ant_sb")
        table_words = keep.tile([P, T], I32, name="table_words", align_bytes=64)
        table_scales = keep.tile([P, T], U8, name="table_scales", align_bytes=64)
        unit_sb = keep.tile([P, TILES], F32, name="unit_sb")
        ident = keep.tile([P, P], F32, name="ident")

        def load_weight(w, first, count, name):
            raw = keep.tile([P, PACK, count], F32, name=name)
            nc.sync.dma_start(out=raw[:], in_=w[:, first : first + count].rearrange("(p j) c -> p j c", j=PACK))
            return raw

        def load_received(r, tiles, name):
            rows = keep.tile([P, len(tiles), S], F32, name=name)
            nc.sync.dma_start(
                out=rows[:], in_=r[tiles[0] * P : (tiles[-1] + 1) * P, :].rearrange("(b p) c -> p b c", p=P)
            )
            return {b: rows[:, n, :] for n, b in enumerate(tiles)}

        nc.gpsimd.memset(table_scales[:].bitcast(I32), 0)
        w1_raw, w2_raw, ra_sb, rb_sb = {}, {}, {}, {}
        nc.sync.dma_start(offs_sb[:], offs)
        w1_raw[0] = load_weight(w1, 0, 128, "w1_raw0")
        w2_raw[0] = load_weight(w2, 0, 128, "w2_raw0")
        for q in range(4):
            nc.sync.dma_start(
                out=table_scales[32 * q : 32 * q + 4, :].bitcast(I32),
                in_=x_scales[0, 4 * q : 4 * q + 4, :].bitcast(I32),
            )
        nc.sync.dma_start(out=table_words[:], in_=x_words[0].rearrange("p n t -> p (n t)").bitcast(I32))
        with nc.allow_non_contiguous_dma(reason="one value a partition and tile"):
            nc.sync.dma_start(out=unit_sb[:], in_=unit.rearrange("(b p) o -> p (b o)", p=P))
        nc.sync.dma_start(ant_sb[:], ant)
        w1_raw[1] = load_weight(w1, 128, 128, "w1_raw1")
        w2_raw[1] = load_weight(w2, 128, 128, "w2_raw1")
        ra_sb.update(load_received(ra, (0,), "ra0"))
        rb_sb.update(load_received(rb, (0,), "rb0"))
        w1_raw[2] = load_weight(w1, 256, 256, "w1_raw2")
        w2_raw[2] = load_weight(w2, 256, 256, "w2_raw2")
        ra_sb.update(load_received(ra, (1,), "ra1"))
        rb_sb.update(load_received(rb, (1,), "rb1"))
        ra_sb.update(load_received(ra, (2, 3,), "ra23"))
        rb_sb.update(load_received(rb, (2, 3,), "rb23"))
        w3_raw = load_weight(w3, 0, N, "w3_raw")
        make_identity(nc, ident[:])
        warm = keep.tile([P, 1], F32, name="warm")
        nc.scalar.activation(warm[:], ident[:, 0:1], ACT.Abs_reciprocal_sqrt, bias=0.3)

        def quantize(grouped, name):
            width = grouped.shape[1] // PACK
            codes = keep.tile([P, width], U32, name=name + "_codes", align_bytes=64)
            scales = keep.tile([P, width], U8, name=name + "_scales", align_bytes=64)
            nc.vector.quantize_mx(out=codes[:].bitcast(FP8X4), scales=scales[:], in_=grouped[:])
            return codes, scales

        def quantize_weight(raw, name, copy):
            grouped = keep.tile([P, PACK * raw.shape[2]], BF16, name=name + "_bf", align_bytes=64)
            copy(
                out=grouped[:].rearrange("p (a i j) -> p a j i", i=4, j=PACK),
                in_=raw[:].rearrange("p j (a i) -> p a j i", i=4),
            )
            return quantize(grouped, name)

        def multiply(bank, weight, first, codes, scales):
            cols = slice(first, first + P)
            nc.tensor.matmul_mx(
                out=bank, lhsT=weight[0][:, cols].bitcast(FP8X4), lhsT_scale=weight[1][:, cols],
                rhs=codes[:].bitcast(FP8X4), rhs_scale=scales[:], start=True, stop=True,
            )

        x_codes = keep.tile([P, S], U32, name="x_codes", align_bytes=64)
        x_bytes = keep.tile([P, S], U8, name="x_bytes", align_bytes=64)
        nc.vector.tensor_copy(x_bytes[:], table_scales[:].indirect(offs_sb[:]))
        nc.vector.tensor_copy(x_codes[:], table_words[:].bitcast(U32).indirect(offs_sb[:]))

        unit_half = keep.tile([P, TILES], F32, name="unit_half")
        unit_quarter = keep.tile([P, TILES], F32, name="unit_quarter")
        nc.vector.tensor_scalar(unit_half[:], unit_sb[:], 0.5, 0.0, ALU.mult, ALU.add)
        nc.vector.tensor_scalar(unit_quarter[:], unit_sb[:], 0.25, 0.0, ALU.mult, ALU.add)

        rows = {}

        def channels(b, wq1, wq2, first):
            hr_ps = psum.tile([P, S], F32, name="hr_ps", tag="product")
            hi_ps = psum.tile([P, S], F32, name="hi_ps", tag="product")
            multiply(hr_ps[:], wq1, first, x_codes, x_bytes)
            multiply(hi_ps[:], wq2, first, x_codes, x_bytes)
            hr = keep.tile([P, S], F32, name="hr%d" % b)
            hi = keep.tile([P, S], F32, name="hi%d" % b)
            hr_sq = work.tile([P, S], F32, name="hr_sq")
            hi_sq = work.tile([P, S], F32, name="hi_sq")
            nc.scalar.activation(hr[:], hr_ps[:], ACT.Copy, scale=unit_half[:, b : b + 1])
            nc.scalar.activation(hr_sq[:], hr_ps[:], ACT.Square)
            nc.scalar.activation(hi_sq[:], hi_ps[:], ACT.Square)
            nc.scalar.activation(hi[:], hi_ps[:], ACT.Copy, scale=unit_quarter[:, b : b + 1])
            own = keep.tile([P, S], F32, name="own%d" % b)
            hr_ra = keep.tile([P, S], F32, name="hr_ra%d" % b)
            hi_rb = keep.tile([P, S], F32, name="hi_rb%d" % b)
            nc.vector.tensor_tensor(own[:], hr_sq[:], hi_sq[:], ALU.add)
            nc.vector.tensor_tensor(hr_ra[:], hr[:], ra_sb[b], ALU.mult)
            nc.vector.scalar_tensor_tensor(hi_rb[:], hi[:], -1.0, rb_sb[b], ALU.mult, ALU.mult)
            return hr, hi, own, hr_ra, hi_rb

        def sums(tiles, first, count, scalar_fetches):
            en = psum.tile([P, len(tiles) * count], F32, name="en", tag="energy")
            ta = psum.tile([P, len(tiles) * count], F32, name="ta", tag="ta")
            tb = psum.tile([P, len(tiles) * count], F32, name="tb", tag="tb")
            terms = {}
            pieces = [(b, j0) for b in tiles for j0 in range(first, first + count, GATHER)]
            for n, (b, j0) in enumerate(pieces):
                hr, hi, own, hr_ra, hi_rb = rows[b]
                width = min(GATHER, first + count - j0)
                cols = slice(j0, j0 + width)
                places = ant_sb[:, j0 // LIST_ROWS : (j0 + width) // LIST_ROWS]
                other = work.tile([P, width], F32, name="other", tag="other%d" % n)
                gr_rb = work.tile([P, width], F32, name="gr_rb", tag="gr_rb%d" % n)
                gi_ra = work.tile([P, width], F32, name="gi_ra", tag="gi_ra%d" % n)
                nc.scalar.activation(other[:], own[:].indirect(places), ACT.Copy)
                if scalar_fetches:
                    gi = work.tile([P, width], F32, name="gi", tag="gi%d" % n)
                    nc.scalar.activation(gi[:], hi[:].indirect(places), ACT.Copy)
                    nc.vector.tensor_tensor(gi_ra[:], gi[:], ra_sb[b][:, cols], ALU.mult)
                else:
                    nc.vector.tensor_tensor(gi_ra[:], hi[:].indirect(places), ra_sb[b][:, cols], ALU.mult)
                nc.vector.tensor_tensor(gr_rb[:], hr[:].indirect(places), rb_sb[b][:, cols], ALU.mult)
                for c in range(0, width, P):
                    near, far = slice(c, c + P), slice(j0 + c, j0 + c + P)
                    place = (j0 + c - first) // P * len(tiles) + tiles.index(b)
                    terms[place] = (
                        [other[:, near], own[:, far]],
                        [gi_ra[:, near], hi_rb[:, far]],
                        [gr_rb[:, near], gi_ra[:, near], hr_ra[:, far]],
                    )
            for k, bank in enumerate((en, tb, ta)):
                for place, block in terms.items():
                    for i, term in enumerate(block[k]):
                        nc.tensor.matmul(
                            out=bank[:, place * P : (place + 1) * P], lhsT=term, rhs=ident[:],
                            is_transpose=True, start=(i == 0), stop=(i == len(block[k]) - 1),
                        )
            return en, ta, tb

        hid_turned = {j0: keep.tile([P, count // P, H], BF16, name="hid_turned%d" % j0) for j0, count in STRETCHES}

        def combine(tiles, first, count, banks):
            en, ta, tb = banks
            features = len(tiles) * P
            root = work.tile([P, len(tiles) * count], F32, name="root")
            part = work.tile([P, len(tiles) * count], F32, name="part")
            both = work.tile([P, len(tiles) * count], F32, name="both")
            nc.scalar.activation(root[:], en[:], ACT.Abs_reciprocal_sqrt, bias=0.3)
            nc.vector.scalar_tensor_tensor(part[:], root[:], -0.25, tb[:], ALU.add, ALU.mult)
            nc.vector.scalar_tensor_tensor(both[:], part[:], 4.0, ta[:], ALU.mult, ALU.add)
            for j0, width in STRETCHES:
                if first <= j0 < first + count:
                    blocks = slice((j0 - first) // P, (j0 - first + width) // P)
                    nc.vector.tensor_tensor(
                        hid_turned[j0][:, :, tiles[0] * P : tiles[0] * P + features],
                        both[:].rearrange("p (n m) -> p n m", m=features)[:, blocks, :],
                        root[:].rearrange("p (n m) -> p n m", m=features)[:, blocks, :],
                        ALU.mult,
                    )

        def streams(first, count, wq3):
            back = psum.tile([P, count // P, 2, P], F32, name="back", tag="product")
            for n in range(count // P):
                words = hid_turned[first][:, n, :].bitcast(F32)
                for u in range(2):
                    nc.tensor.transpose(back[:, n, u, :], words[:, u : H // 2 : 2], ident[:])
            grouped = keep.tile([P, PACK * count], BF16, name="hid_bf%d" % first, align_bytes=64)
            nc.scalar.copy(
                out=grouped[:].bitcast(F32).rearrange("p (n j u) -> p n j u", j=P, u=2),
                in_=back[:].rearrange("p n u j -> p n j u"),
            )
            codes, scales = quantize(grouped, "hid%d" % first)
            acc = psum.tile([P, N // P, count], F32, name="acc", tag="product")
            for m in range(N // P):
                multiply(acc[:, m, :], wq3, m * P, codes, scales)
            result = keep.tile([P, N // P, count], F32, name="result%d" % first)
            nc.vector.tensor_copy(out=result[:], in_=acc[:])
            nc.sync.dma_start(out=out[:, first : first + count].rearrange("(m p) j -> p m j", p=P), in_=result[:])

        wq1_0 = quantize_weight(w1_raw[0], "w1_0", nc.vector.tensor_copy)
        wq2_0 = quantize_weight(w2_raw[0], "w2_0", nc.vector.tensor_copy)
        wq1_1 = quantize_weight(w1_raw[1], "w1_1", nc.vector.tensor_copy)
        wq2_1 = quantize_weight(w2_raw[1], "w2_1", nc.vector.tensor_copy)
        rows[0] = channels(0, wq1_0, wq2_0, 0)
        m0_0 = sums([0], 0, S, False)
        rows[1] = channels(1, wq1_1, wq2_1, 0)
        wq1_2 = quantize_weight(w1_raw[2], "w1_2", nc.scalar.copy)
        wq2_2 = quantize_weight(w2_raw[2], "w2_2", nc.scalar.copy)
        wq3 = quantize_weight(w3_raw, "w3", nc.scalar.copy)
        combine([0], 0, S, m0_0)
        rows[2] = channels(2, wq1_2, wq2_2, 0)
        m1_0 = sums([1], 0, S, False)
        rows[3] = channels(3, wq1_2, wq2_2, 128)
        combine([1], 0, S, m1_0)
        m23_0 = sums([2, 3], 0, 256, False)
        combine([2, 3], 0, 256, m23_0)
        m23_256 = sums([2, 3], 256, 128, False)
        streams(STRETCHES[0][0], STRETCHES[0][1], wq3)
        combine([2, 3], 256, 128, m23_256)
        m23_384 = sums([2, 3], 384, 128, False)
        streams(STRETCHES[1][0], STRETCHES[1][1], wq3)
        combine([2, 3], 384, 128, m23_384)
        streams(STRETCHES[2][0], STRETCHES[2][1], wq3)
